import numpy as np
import ml_dtypes


def mxq(x, axis, fmt="e4m3"):
    dtype, down = {"e4m3": (ml_dtypes.float8_e4m3fn, 7), "e5m2": (ml_dtypes.float8_e5m2, 14)}[fmt]
    v = np.moveaxis(np.asarray(x, np.float32).astype(ml_dtypes.bfloat16).astype(np.float64), axis, -1)
    blocks = v.reshape(v.shape[:-1] + (-1, 32))
    amax = np.abs(blocks).max(-1, keepdims=True)
    byte = np.maximum(np.where(amax > 0, np.frexp(amax)[1] - 1 + 127, 0) - down, 1)
    scale = np.exp2(byte - 127.0)
    codes = (blocks / scale).astype(np.float32).astype(dtype).astype(np.float64)
    return np.moveaxis((codes * scale).reshape(v.shape), -1, axis)


WIDE = False


def mx_kscale(k):
    if not WIDE:
        return np.ones(k)
    levels = np.array([10, -10, 5, -5, 0])
    if k % 512:
        return np.exp2(np.random.permutation(np.resize(levels, k // 32))).repeat(32)
    a = np.empty((k // 512, 16))
    for p in range(k // 512):
        a[p, :8] = np.random.permutation(np.resize(levels, 8))
        for g in range(8):
            far = levels[np.abs(levels - a[p, g]) >= 10]
            a[p, g + 8] = far[np.random.randint(len(far))]
    return np.exp2(a.ravel()).repeat(32)


def f64(x):
    return np.asarray(x).astype(np.float64)


def striped(idx):
    return np.tile(np.asarray(idx).reshape(-1, 16).T, (8, 1)).astype(np.uint16)


def unstriped(offs):
    return offs[:16].T.reshape(-1).astype(np.int64)


E2M1 = np.array([0.0, 0.5, 1.0, 1.5, 2.0, 3.0, 4.0, 6.0, -0.0, -0.5, -1.0, -1.5, -2.0, -3.0, -4.0, -6.0])


def pack_weight(w, fmt):
    k, n = w.shape
    w = f64(np.asarray(w, np.float32).astype(ml_dtypes.bfloat16)).reshape(k // 32, 32, n)
    amax = np.abs(w).max(1)
    if fmt == "e4m3":
        byte = np.frexp(amax)[1] - 1 + 127 - 7
    else:
        mant, ex = np.frexp(amax / 6.0)
        byte = np.where(mant > 0.5, ex, ex - 1) + 127
    byte = np.clip(np.where(amax > 0, byte, 1), 1, 254)
    scaled = (w * np.exp2(127.0 - byte)[:, None, :]).reshape(k, n).astype(np.float32)
    by_word = np.ascontiguousarray(scaled.reshape(k // 512, 128, 4, n).transpose(0, 1, 3, 2))
    if fmt == "e4m3":
        words = by_word.astype(ml_dtypes.float8_e4m3fn).view(np.uint8)
    else:
        c = by_word.astype(ml_dtypes.float4_e2m1fn).view(np.uint8) & 0xF
        words = (c[..., 0::2] | (c[..., 1::2] << 4)).reshape(k // 512, 128, 2 * n)
    return np.ascontiguousarray(words), np.ascontiguousarray(byte.astype(np.uint8).reshape(k // 512, 16, n))


def unpack_weight(words, scales, fmt):
    g, _, n = scales.shape
    words = np.ascontiguousarray(words).reshape(g, 128, n, -1)
    if fmt == "e4m3":
        vals = words.view(ml_dtypes.float8_e4m3fn).astype(np.float64)
    else:
        nib = np.empty((g, 128, n, 4), np.uint8)
        nib[..., 0::2] = words & 0xF
        nib[..., 1::2] = words >> 4
        vals = E2M1[nib]
    vals = vals * np.repeat(np.exp2(scales.astype(np.float64) - 127.0), 8, axis=1)[..., None]
    return vals.transpose(0, 1, 3, 2).reshape(g * 512, n)


D, E, T, I, G, U, Q = 512, 512, 2048, 512, 64, 512, 128


def setup_inputs():
    n = np.random.standard_normal
    idx = np.random.permutation(T)[:I]
    idx2 = np.random.permutation(U)[:G]
    fd = mx_kscale(D)
    fe = mx_kscale(E)
    pgsump = pack_weight(n((D, U)) / fd[:, None], "e4m3")
    keysp = pack_weight(n((D, T)) / fd[:, None], "e4m3")
    valsp = pack_weight(n((E, T)) / fe[:, None], "e4m3")
    return {
        "pquery": (n((D, Q)) * 1.0 / np.sqrt(D) * fd[:, None]).astype(np.float32),
        "pgsum_words": pgsump[0],
        "pgsum_scales": pgsump[1],
        "query": (n((D, Q)) * 0.7 / np.sqrt(D) * fd[:, None]).astype(np.float32),
        "keys_words": keysp[0],
        "keys_scales": keysp[1],
        "even": (np.random.uniform(0.1, 0.6, (Q, 1))).astype(np.float32),
        "gout": (n((E, Q)) * 1 / np.sqrt(E) * fe[:, None]).astype(np.float32),
        "vals_words": valsp[0],
        "vals_scales": valsp[1],
        "old": (0.5 * n((Q, U))).astype(np.float32),
        "offs": striped(idx),
        "offs2": striped(idx2),
    }


def reference(pquery, pgsum_words, pgsum_scales, query, keys_words, keys_scales, even, gout, vals_words, vals_scales, old, offs, offs2):
    idx = unstriped(offs)
    idx2 = unstriped(offs2)
    pgsumu = unpack_weight(pgsum_words, pgsum_scales, "e4m3")
    keysu = unpack_weight(keys_words, keys_scales, "e4m3")
    valsu = unpack_weight(vals_words, vals_scales, "e4m3")
    pqueryq = mxq(f64(pquery), 0, "e4m3")
    pgsumidx2g = pgsumu[:, idx2]
    b = pqueryq.T @ pgsumidx2g
    pb = np.exp(b - np.max(b, axis=1, keepdims=True))
    zb = np.sum(pb, axis=1, keepdims=True)
    queryq = mxq(f64(query), 0, "e4m3")
    keysidxg = keysu[:, idx]
    a = queryq.T @ keysidxg
    pa = np.exp(a)
    s = pa.reshape(Q, G, I // G).sum(axis=2)
    goutq = mxq(f64(gout), 0, "e4m3")
    valsidxg = valsu[:, idx]
    c0 = goutq.T @ valsidxg
    m1 = (pa * c0).reshape(Q, G, I // G).sum(axis=2) / s
    dzb = np.sum(m1 * (1.0 - f64(even)) * pb / np.square(zb) * (-1.0), axis=1, keepdims=True)
    dpb = m1 * (1.0 - f64(even)) / zb + dzb
    db = dpb * pb
    gs = db * 256.0
    gf = np.zeros((Q, U))
    gf[:, idx2] = gs
    y = f64(old) + gf
    return y

@@ -1,0 +1,151 @@
+from contextlib import ExitStack
+
+import concourse.mybir as mybir
+
+D, E, T, I, G, U, Q = 512, 512, 2048, 512, 64, 512, 128
+FLOPS = 2 * Q * (D * G + D * I + E * I)
+
+F32 = mybir.dt.float32
+BF16 = mybir.dt.bfloat16
+I32 = mybir.dt.int32
+U32 = mybir.dt.uint32
+U16 = mybir.dt.uint16
+U8 = mybir.dt.uint8
+FP8X4 = mybir.dt.float8_e4m3fn_x4
+ALU = mybir.AluOpType
+ACT = mybir.ActivationFunctionType
+AX = mybir.AxisListType
+
+P = 128
+PACK = 4
+PAGE = I // G
+
+
+def tile_attend_bevenmass_b_kernel(tc, pquery, pgsum_words, pgsum_scales, query, keys_words, keys_scales,
+                                    even, gout, vals_words, vals_scales, old, offs, offs2, out):
+    nc = tc.nc
+    with ExitStack() as ctx:
+        sb = ctx.enter_context(tc.tile_pool(name="sb", bufs=1))
+        ps = ctx.enter_context(tc.psum_pool(name="ps", bufs=1))
+
+        def tile(shape, dtype, name, tag=None):
+            return sb.tile(shape, dtype, name=name, tag=tag or name, align_bytes=64)
+
+        lst = tile([P, I // 16], U16, "lst")
+        lst2 = tile([P, G // 16], U16, "lst2")
+        kw = tile([P, T], U32, "kw")
+        vw = tile([P, T], U32, "vw")
+        pw = tile([P, U], U32, "pw")
+        ks = tile([P, T], U8, "ks")
+        vs = tile([P, T], U8, "vs")
+        pgs = tile([P, U], U8, "pgs")
+        q_raw = tile([P, PACK, Q], F32, "q_raw")
+        p_raw = tile([P, PACK, Q], F32, "p_raw")
+        g_raw = tile([P, PACK, Q], F32, "g_raw")
+        ev = tile([P, 1], F32, "ev")
+        old_sb = tile([P, U], F32, "old_sb")
+        gf = tile([P, U], F32, "gf")
+        warm = tile([P, 1], F32, "warm")
+
+        def load_words(queue, dst, src):
+            queue.dma_start(out=dst[:].bitcast(I32), in_=src[0].rearrange("p n t -> p (n t)").bitcast(I32))
+
+        def load_rows(queue, dst, src):
+            queue.dma_start(out=dst[:], in_=src.rearrange("(p j) w -> p j w", j=PACK))
+
+        def load_scales(queue, dst, src, first):
+            rows = src[0].rearrange("(a r) n -> r a n", r=4)
+            for r in range(4):
+                queue.dma_start(out=dst[first + r:P:32, :].bitcast(I32), in_=rows[r].bitcast(I32))
+
+        nc.vector.memset(ks[:, 0:T // 2].bitcast(I32), 0)
+        nc.gpsimd.memset(ks[:, T // 2:T].bitcast(I32), 0)
+        nc.gpsimd.memset(warm[:], 0.0)
+        nc.vector.memset(vs[:].bitcast(I32), 0)
+        nc.vector.memset(pgs[:].bitcast(I32), 0)
+        nc.vector.memset(gf[:], 0.0)
+
+        nc.sync.dma_start(lst[:], offs)
+        load_words(nc.scalar, kw, keys_words)
+        warm2 = tile([P, 1], F32, "warm2")
+        nc.scalar.activation(warm2[:], warm[:], ACT.Exp)
+        load_scales(nc.sync, ks, keys_scales, 0)
+        nc.sync.dma_start(lst2[:], offs2)
+        load_rows(nc.sync, q_raw, query)
+        load_rows(nc.sync, p_raw, pquery)
+        load_scales(nc.sync, vs, vals_scales, 4)
+        load_rows(nc.sync, g_raw, gout)
+        load_words(nc.sync, pw, pgsum_words)
+        load_scales(nc.sync, pgs, pgsum_scales, 0)
+        load_words(nc.sync, vw, vals_words)
+        nc.sync.dma_start(out=ev[:], in_=even)
+        nc.sync.dma_start(out=old_sb[:], in_=old)
+
+        def quantise(raws, name):
+            n = len(raws)
+            grouped = tile([P, n, Q, PACK], BF16, name + "_bf")
+            codes = tile([P, n * Q], U32, name + "_codes")
+            scales = tile([P, n * Q], U8, name + "_scales")
+            for j in range(n):
+                nc.scalar.copy(out=grouped[:, j].rearrange("p (c i) t -> p c t i", i=4),
+                               in_=raws[j][:].rearrange("p t (c i) -> p c t i", i=4))
+            nc.vector.quantize_mx(out=codes[:].bitcast(FP8X4), scales=scales[:],
+                                  in_=grouped[:].rearrange("p n w j -> p (n w j)"))
+            return codes, scales
+
+        ks_g = tile([P, I], U8, "ks_g")
+        vs_g = tile([P, I], U8, "vs_g")
+        kw_g = tile([P, I], U32, "kw_g")
+        nc.vector.tensor_copy(ks_g[:], ks[:].indirect(lst[:]))
+        nc.vector.tensor_copy(kw_g[:], kw[:].indirect(lst[:]))
+        q_codes, q_scales = quantise([q_raw], "q")
+        a_ps = ps.tile([P, I], F32, name="a_ps")
+        nc.tensor.matmul_mx(out=a_ps[:], lhsT=q_codes[:].bitcast(FP8X4), lhsT_scale=q_scales[:],
+                            rhs=kw_g[:].bitcast(FP8X4), rhs_scale=ks_g[:], start=True, stop=True)
+        pa = tile([P, I], F32, "pa")
+        nc.scalar.activation(pa[:], a_ps[:], ACT.Exp)
+        nc.vector.tensor_copy(vs_g[:], vs[:].indirect(lst[:]))
+
+        pg_codes, pg_scales = quantise([p_raw, g_raw], "pg")
+        pw_g = tile([P, G], U32, "pw_g")
+        pgs_g = tile([P, G], U8, "pgs_g")
+        nc.vector.tensor_copy(pw_g[:], pw[:].indirect(lst2[:]))
+        nc.vector.tensor_copy(pgs_g[:], pgs[:].indirect(lst2[:]))
+        b_ps = ps.tile([P, G], F32, name="b_ps")
+        nc.tensor.matmul_mx(out=b_ps[:], lhsT=pg_codes[:, 0:Q].bitcast(FP8X4), lhsT_scale=pg_scales[:, 0:Q],
+                            rhs=pw_g[:].bitcast(FP8X4), rhs_scale=pgs_g[:], start=True, stop=True)
+        sums = tile([P, G + 1], F32, "sums")
+        nc.vector.tensor_reduce(sums[:, 0:G], pa[:].rearrange("p (g r) -> p g r", r=PAGE), AX.X, ALU.add)
+        negmax = tile([P, 1], F32, "negmax")
+        nc.vector.tensor_reduce(negmax[:], b_ps[:], AX.X, ALU.max, negate=True)
+        pb = tile([P, G], F32, "pb")
+        nc.scalar.activation(pb[:], b_ps[:], ACT.Exp, bias=negmax[:], accum_out=sums[:, G:G + 1])
+        gain = tile([P, 1], F32, "gain")
+        nc.scalar.activation(gain[:], ev[:], ACT.Copy, bias=256.0, scale=-256.0)
+
+        vw_g = tile([P, I], U32, "vw_g")
+        nc.vector.tensor_copy(vw_g[:], vw[:].indirect(lst[:]))
+        c_ps = ps.tile([P, I], F32, name="c_ps")
+        nc.tensor.matmul_mx(out=c_ps[:], lhsT=pg_codes[:, Q:2 * Q].bitcast(FP8X4), lhsT_scale=pg_scales[:, Q:2 * Q],
+                            rhs=vw_g[:].bitcast(FP8X4), rhs_scale=vs_g[4:P, :], start=True, stop=True)
+        inv = tile([P, G + 1], F32, "inv", tag="vw")
+        nc.vector.reciprocal(inv[:], sums[:])
+        ratio = tile([P, G], F32, "ratio")
+        nc.gpsimd.tensor_tensor(ratio[:], pb[:], inv[:, 0:G], ALU.mult)
+        gain_z = tile([P, 1], F32, "gain_z")
+        nc.scalar.activation(gain_z[:], inv[:, G:G + 1], ACT.Copy, scale=gain[:])
+        neg_z = tile([P, 1], F32, "neg_z")
+        nc.scalar.activation(neg_z[:], inv[:, G:G + 1], ACT.Copy, scale=-1.0)
+        wc = tile([P, I], F32, "wc")
+        nc.vector.tensor_tensor(wc[:], c_ps[:], pa[:], ALU.mult)
+        num = tile([P, G], F32, "num")
+        nc.vector.tensor_reduce(num[:], wc[:].rearrange("p (g r) -> p g r", r=PAGE), AX.X, ALU.add)
+        part = tile([P, G], F32, "part")
+        total = tile([P, 1], F32, "total")
+        nc.vector.scalar_tensor_tensor(part[:], num[:], gain_z[:], ratio[:], ALU.mult, ALU.mult, accum_out=total[:])
+        back = tile([P, G], F32, "back")
+        nc.vector.tensor_scalar(back[:], pb[:], total[:], neg_z[:], ALU.mult, ALU.mult)
+        nc.vector.tensor_tensor(gf[:].indirect(lst2[:]), part[:], back[:], ALU.add)
+        res = tile([P, U], F32, "res")
+        nc.vector.tensor_tensor(res[:], old_sb[:], gf[:], ALU.add)
+        nc.sync.dma_start(out=out, in_=res[:])

@@ -33,19 +33,18 @@ def tile_attend_bevenmass_b_kernel(tc, pquery, pgsum_words, pgsum_scales, query,
 
         lst = tile([P, I // 16], U16, "lst")
         lst2 = tile([P, G // 16], U16, "lst2")
-        kw = tile([P, T], U32, "kw")
-        vw = tile([P, T], U32, "vw")
-        pw = tile([P, U], U32, "pw")
         ks = tile([P, T], U8, "ks")
         vs = tile([P, T], U8, "vs")
         pgs = tile([P, U], U8, "pgs")
+        kw = tile([P, T], U32, "kw")
+        vw = tile([P, T], U32, "vw")
+        pw = tile([P, U], U32, "pw")
         q_raw = tile([P, PACK, Q], F32, "q_raw")
         p_raw = tile([P, PACK, Q], F32, "p_raw")
         g_raw = tile([P, PACK, Q], F32, "g_raw")
-        ev = tile([P, 1], F32, "ev")
         old_sb = tile([P, U], F32, "old_sb")
+        ev = tile([P, 1], F32, "ev")
         gf = tile([P, U], F32, "gf")
-        warm = tile([P, 1], F32, "warm")
 
         def load_words(queue, dst, src):
             queue.dma_start(out=dst[:].bitcast(I32), in_=src[0].rearrange("p n t -> p (n t)").bitcast(I32))
@@ -53,38 +52,35 @@ def tile_attend_bevenmass_b_kernel(tc, pquery, pgsum_words, pgsum_scales, query,
         def load_rows(queue, dst, src):
             queue.dma_start(out=dst[:], in_=src.rearrange("(p j) w -> p j w", j=PACK))
 
-        def load_scales(queue, dst, src, first):
+        def load_scales(queues, dst, src, first):
             rows = src[0].rearrange("(a r) n -> r a n", r=4)
             for r in range(4):
-                queue.dma_start(out=dst[first + r:P:32, :].bitcast(I32), in_=rows[r].bitcast(I32))
+                queues[r % len(queues)].dma_start(out=dst[first + r:P:32, :].bitcast(I32), in_=rows[r].bitcast(I32))
 
         nc.vector.memset(ks[:, 0:T // 2].bitcast(I32), 0)
         nc.gpsimd.memset(ks[:, T // 2:T].bitcast(I32), 0)
-        nc.gpsimd.memset(warm[:], 0.0)
         nc.vector.memset(vs[:].bitcast(I32), 0)
         nc.vector.memset(pgs[:].bitcast(I32), 0)
-        nc.vector.memset(gf[:], 0.0)
+        nc.gpsimd.memset(gf[:], 0.0)
 
         nc.sync.dma_start(lst[:], offs)
-        load_words(nc.scalar, kw, keys_words)
-        warm2 = tile([P, 1], F32, "warm2")
-        nc.scalar.activation(warm2[:], warm[:], ACT.Exp)
-        load_scales(nc.sync, ks, keys_scales, 0)
-        nc.sync.dma_start(lst2[:], offs2)
         load_rows(nc.sync, q_raw, query)
-        load_rows(nc.sync, p_raw, pquery)
-        load_scales(nc.sync, vs, vals_scales, 4)
+        load_scales((nc.sync, nc.scalar), ks, keys_scales, 0)
+        load_words(nc.sync, kw, keys_words)
+        load_scales((nc.sync,), vs, vals_scales, 4)
         load_rows(nc.sync, g_raw, gout)
-        load_words(nc.sync, pw, pgsum_words)
-        load_scales(nc.sync, pgs, pgsum_scales, 0)
         load_words(nc.sync, vw, vals_words)
+        load_rows(nc.sync, p_raw, pquery)
+        nc.sync.dma_start(lst2[:], offs2)
+        load_scales((nc.sync,), pgs, pgsum_scales, 0)
+        load_words(nc.sync, pw, pgsum_words)
         nc.sync.dma_start(out=ev[:], in_=even)
         nc.sync.dma_start(out=old_sb[:], in_=old)
 
-        def quantise(raws, name):
+        def quantise(raws, name, after=None):
             n = len(raws)
             grouped = tile([P, n, Q, PACK], BF16, name + "_bf")
-            codes = tile([P, n * Q], U32, name + "_codes")
+            codes = tile([P, n * Q], U32, name + "_codes", tag=after)
             scales = tile([P, n * Q], U8, name + "_scales")
             for j in range(n):
                 nc.scalar.copy(out=grouped[:, j].rearrange("p (c i) t -> p c t i", i=4),
@@ -95,26 +91,33 @@ def tile_attend_bevenmass_b_kernel(tc, pquery, pgsum_words, pgsum_scales, query,
 
         ks_g = tile([P, I], U8, "ks_g")
         vs_g = tile([P, I], U8, "vs_g")
-        kw_g = tile([P, I], U32, "kw_g")
         nc.vector.tensor_copy(ks_g[:], ks[:].indirect(lst[:]))
+        q_codes, q_scales = quantise([q_raw], "q", after="ks")
+        kw_g = tile([P, I], U32, "kw_g")
         nc.vector.tensor_copy(kw_g[:], kw[:].indirect(lst[:]))
-        q_codes, q_scales = quantise([q_raw], "q")
         a_ps = ps.tile([P, I], F32, name="a_ps")
         nc.tensor.matmul_mx(out=a_ps[:], lhsT=q_codes[:].bitcast(FP8X4), lhsT_scale=q_scales[:],
                             rhs=kw_g[:].bitcast(FP8X4), rhs_scale=ks_g[:], start=True, stop=True)
-        pa = tile([P, I], F32, "pa")
-        nc.scalar.activation(pa[:], a_ps[:], ACT.Exp)
         nc.vector.tensor_copy(vs_g[:], vs[:].indirect(lst[:]))
+        g_codes, g_scales = quantise([g_raw], "g")
+        pa = tile([P, I], F32, "pa", tag="g_raw")
+        nc.scalar.activation(pa[:], a_ps[:], ACT.Exp)
 
-        pg_codes, pg_scales = quantise([p_raw, g_raw], "pg")
+        vw_g = tile([P, I], U32, "vw_g")
+        nc.vector.tensor_copy(vw_g[:], vw[:].indirect(lst[:]))
+        c_ps = ps.tile([P, I], F32, name="c_ps")
+        nc.tensor.matmul_mx(out=c_ps[:], lhsT=g_codes[:].bitcast(FP8X4), lhsT_scale=g_scales[:],
+                            rhs=vw_g[:].bitcast(FP8X4), rhs_scale=vs_g[4:P, :], start=True, stop=True)
+
+        p_codes, p_scales = quantise([p_raw], "p")
         pw_g = tile([P, G], U32, "pw_g")
         pgs_g = tile([P, G], U8, "pgs_g")
-        nc.vector.tensor_copy(pw_g[:], pw[:].indirect(lst2[:]))
         nc.vector.tensor_copy(pgs_g[:], pgs[:].indirect(lst2[:]))
+        nc.vector.tensor_copy(pw_g[:], pw[:].indirect(lst2[:]))
         b_ps = ps.tile([P, G], F32, name="b_ps")
-        nc.tensor.matmul_mx(out=b_ps[:], lhsT=pg_codes[:, 0:Q].bitcast(FP8X4), lhsT_scale=pg_scales[:, 0:Q],
+        nc.tensor.matmul_mx(out=b_ps[:], lhsT=p_codes[:].bitcast(FP8X4), lhsT_scale=p_scales[:],
                             rhs=pw_g[:].bitcast(FP8X4), rhs_scale=pgs_g[:], start=True, stop=True)
-        sums = tile([P, G + 1], F32, "sums")
+        sums = tile([P, G + 1], F32, "sums", tag="pw")
         nc.vector.tensor_reduce(sums[:, 0:G], pa[:].rearrange("p (g r) -> p g r", r=PAGE), AX.X, ALU.add)
         negmax = tile([P, 1], F32, "negmax")
         nc.vector.tensor_reduce(negmax[:], b_ps[:], AX.X, ALU.max, negate=True)
@@ -122,13 +125,8 @@ def tile_attend_bevenmass_b_kernel(tc, pquery, pgsum_words, pgsum_scales, query,
         nc.scalar.activation(pb[:], b_ps[:], ACT.Exp, bias=negmax[:], accum_out=sums[:, G:G + 1])
         gain = tile([P, 1], F32, "gain")
         nc.scalar.activation(gain[:], ev[:], ACT.Copy, bias=256.0, scale=-256.0)
-
-        vw_g = tile([P, I], U32, "vw_g")
-        nc.vector.tensor_copy(vw_g[:], vw[:].indirect(lst[:]))
-        c_ps = ps.tile([P, I], F32, name="c_ps")
-        nc.tensor.matmul_mx(out=c_ps[:], lhsT=pg_codes[:, Q:2 * Q].bitcast(FP8X4), lhsT_scale=pg_scales[:, Q:2 * Q],
-                            rhs=vw_g[:].bitcast(FP8X4), rhs_scale=vs_g[4:P, :], start=True, stop=True)
-        inv = tile([P, G + 1], F32, "inv", tag="vw")
+        nc.vector.tensor_tensor(pa[:], c_ps[:], pa[:], ALU.mult)
+        inv = tile([P, G + 1], F32, "inv")
         nc.vector.reciprocal(inv[:], sums[:])
         ratio = tile([P, G], F32, "ratio")
         nc.gpsimd.tensor_tensor(ratio[:], pb[:], inv[:, 0:G], ALU.mult)
@@ -136,10 +134,8 @@ def tile_attend_bevenmass_b_kernel(tc, pquery, pgsum_words, pgsum_scales, query,
         nc.scalar.activation(gain_z[:], inv[:, G:G + 1], ACT.Copy, scale=gain[:])
         neg_z = tile([P, 1], F32, "neg_z")
         nc.scalar.activation(neg_z[:], inv[:, G:G + 1], ACT.Copy, scale=-1.0)
-        wc = tile([P, I], F32, "wc")
-        nc.vector.tensor_tensor(wc[:], c_ps[:], pa[:], ALU.mult)
         num = tile([P, G], F32, "num")
-        nc.vector.tensor_reduce(num[:], wc[:].rearrange("p (g r) -> p g r", r=PAGE), AX.X, ALU.add)
+        nc.vector.tensor_reduce(num[:], pa[:].rearrange("p (g r) -> p g r", r=PAGE), AX.X, ALU.add)
         part = tile([P, G], F32, "part")
         total = tile([P, 1], F32, "total")
         nc.vector.scalar_tensor_tensor(part[:], num[:], gain_z[:], ratio[:], ALU.mult, ALU.mult, accum_out=total[:])
@@ -147,5 +143,7 @@ def tile_attend_bevenmass_b_kernel(tc, pquery, pgsum_words, pgsum_scales, query,
         nc.vector.tensor_scalar(back[:], pb[:], total[:], neg_z[:], ALU.mult, ALU.mult)
         nc.vector.tensor_tensor(gf[:].indirect(lst2[:]), part[:], back[:], ALU.add)
         res = tile([P, U], F32, "res")
-        nc.vector.tensor_tensor(res[:], old_sb[:], gf[:], ALU.add)
-        nc.sync.dma_start(out=out, in_=res[:])
+        for h, queue in enumerate((nc.sync, nc.scalar)):
+            cols = slice(h * U // 2, (h + 1) * U // 2)
+            nc.vector.tensor_tensor(res[:, cols], old_sb[:, cols], gf[:, cols], ALU.add)
+            queue.dma_start(out=out[:, cols], in_=res[:, cols])

from contextlib import ExitStack

import concourse.mybir as mybir

D, E, T, I, G, U, Q = 512, 512, 2048, 512, 64, 512, 128
FLOPS = 2 * Q * (D * G + D * I + E * I)

F32 = mybir.dt.float32
BF16 = mybir.dt.bfloat16
I32 = mybir.dt.int32
U32 = mybir.dt.uint32
U16 = mybir.dt.uint16
U8 = mybir.dt.uint8
FP8X4 = mybir.dt.float8_e4m3fn_x4
ALU = mybir.AluOpType
ACT = mybir.ActivationFunctionType
AX = mybir.AxisListType

P = 128
PACK = 4
PAGE = I // G


def tile_attend_bevenmass_b_kernel(tc, pquery, pgsum_words, pgsum_scales, query, keys_words, keys_scales,
                                    even, gout, vals_words, vals_scales, old, offs, offs2, out):
    nc = tc.nc
    with ExitStack() as ctx:
        sb = ctx.enter_context(tc.tile_pool(name="sb", bufs=1))
        ps = ctx.enter_context(tc.psum_pool(name="ps", bufs=1))

        def tile(shape, dtype, name, tag=None):
            return sb.tile(shape, dtype, name=name, tag=tag or name, align_bytes=64)

        lst = tile([P, I // 16], U16, "lst")
        lst2 = tile([P, G // 16], U16, "lst2")
        ks = tile([P, T], U8, "ks")
        vs = tile([P, T], U8, "vs")
        pgs = tile([P, U], U8, "pgs")
        kw = tile([P, T], U32, "kw")
        vw = tile([P, T], U32, "vw")
        pw = tile([P, U], U32, "pw")
        q_raw = tile([P, PACK, Q], F32, "q_raw")
        p_raw = tile([P, PACK, Q], F32, "p_raw")
        g_raw = tile([P, PACK, Q], F32, "g_raw")
        old_sb = tile([P, U], F32, "old_sb")
        ev = tile([P, 1], F32, "ev")
        gf = tile([P, U], F32, "gf")

        def load_words(queue, dst, src):
            queue.dma_start(out=dst[:].bitcast(I32), in_=src[0].rearrange("p n t -> p (n t)").bitcast(I32))

        def load_rows(queue, dst, src):
            queue.dma_start(out=dst[:], in_=src.rearrange("(p j) w -> p j w", j=PACK))

        def load_scales(queues, dst, src, first):
            rows = src[0].rearrange("(a r) n -> r a n", r=4)
            for r in range(4):
                queues[r % len(queues)].dma_start(out=dst[first + r:P:32, :].bitcast(I32), in_=rows[r].bitcast(I32))

        nc.vector.memset(ks[:, 0:T // 2].bitcast(I32), 0)
        nc.gpsimd.memset(ks[:, T // 2:T].bitcast(I32), 0)
        nc.vector.memset(vs[:].bitcast(I32), 0)
        nc.vector.memset(pgs[:].bitcast(I32), 0)
        nc.gpsimd.memset(gf[:], 0.0)

        nc.sync.dma_start(lst[:], offs)
        load_rows(nc.sync, q_raw, query)
        load_scales((nc.sync, nc.scalar), ks, keys_scales, 0)
        load_words(nc.sync, kw, keys_words)
        load_scales((nc.sync,), vs, vals_scales, 4)
        load_rows(nc.sync, g_raw, gout)
        load_words(nc.sync, vw, vals_words)
        load_rows(nc.sync, p_raw, pquery)
        nc.sync.dma_start(lst2[:], offs2)
        load_scales((nc.sync,), pgs, pgsum_scales, 0)
        load_words(nc.sync, pw, pgsum_words)
        nc.sync.dma_start(out=ev[:], in_=even)
        nc.sync.dma_start(out=old_sb[:], in_=old)

        def quantise(raws, name, after=None):
            n = len(raws)
            grouped = tile([P, n, Q, PACK], BF16, name + "_bf")
            codes = tile([P, n * Q], U32, name + "_codes", tag=after)
            scales = tile([P, n * Q], U8, name + "_scales")
            for j in range(n):
                nc.scalar.copy(out=grouped[:, j].rearrange("p (c i) t -> p c t i", i=4),
                               in_=raws[j][:].rearrange("p t (c i) -> p c t i", i=4))
            nc.vector.quantize_mx(out=codes[:].bitcast(FP8X4), scales=scales[:],
                                  in_=grouped[:].rearrange("p n w j -> p (n w j)"))
            return codes, scales

        ks_g = tile([P, I], U8, "ks_g")
        vs_g = tile([P, I], U8, "vs_g")
        nc.vector.tensor_copy(ks_g[:], ks[:].indirect(lst[:]))
        q_codes, q_scales = quantise([q_raw], "q", after="ks")
        kw_g = tile([P, I], U32, "kw_g")
        nc.vector.tensor_copy(kw_g[:], kw[:].indirect(lst[:]))
        a_ps = ps.tile([P, I], F32, name="a_ps")
        nc.tensor.matmul_mx(out=a_ps[:], lhsT=q_codes[:].bitcast(FP8X4), lhsT_scale=q_scales[:],
                            rhs=kw_g[:].bitcast(FP8X4), rhs_scale=ks_g[:], start=True, stop=True)
        nc.vector.tensor_copy(vs_g[:], vs[:].indirect(lst[:]))
        g_codes, g_scales = quantise([g_raw], "g")
        pa = tile([P, I], F32, "pa", tag="g_raw")
        nc.scalar.activation(pa[:], a_ps[:], ACT.Exp)

        vw_g = tile([P, I], U32, "vw_g")
        nc.vector.tensor_copy(vw_g[:], vw[:].indirect(lst[:]))
        c_ps = ps.tile([P, I], F32, name="c_ps")
        nc.tensor.matmul_mx(out=c_ps[:], lhsT=g_codes[:].bitcast(FP8X4), lhsT_scale=g_scales[:],
                            rhs=vw_g[:].bitcast(FP8X4), rhs_scale=vs_g[4:P, :], start=True, stop=True)

        p_codes, p_scales = quantise([p_raw], "p")
        pw_g = tile([P, G], U32, "pw_g")
        pgs_g = tile([P, G], U8, "pgs_g")
        nc.vector.tensor_copy(pgs_g[:], pgs[:].indirect(lst2[:]))
        nc.vector.tensor_copy(pw_g[:], pw[:].indirect(lst2[:]))
        b_ps = ps.tile([P, G], F32, name="b_ps")
        nc.tensor.matmul_mx(out=b_ps[:], lhsT=p_codes[:].bitcast(FP8X4), lhsT_scale=p_scales[:],
                            rhs=pw_g[:].bitcast(FP8X4), rhs_scale=pgs_g[:], start=True, stop=True)
        sums = tile([P, G + 1], F32, "sums", tag="pw")
        nc.vector.tensor_reduce(sums[:, 0:G], pa[:].rearrange("p (g r) -> p g r", r=PAGE), AX.X, ALU.add)
        negmax = tile([P, 1], F32, "negmax")
        nc.vector.tensor_reduce(negmax[:], b_ps[:], AX.X, ALU.max, negate=True)
        pb = tile([P, G], F32, "pb")
        nc.scalar.activation(pb[:], b_ps[:], ACT.Exp, bias=negmax[:], accum_out=sums[:, G:G + 1])
        gain = tile([P, 1], F32, "gain")
        nc.scalar.activation(gain[:], ev[:], ACT.Copy, bias=256.0, scale=-256.0)
        nc.vector.tensor_tensor(pa[:], c_ps[:], pa[:], ALU.mult)
        inv = tile([P, G + 1], F32, "inv")
        nc.vector.reciprocal(inv[:], sums[:])
        ratio = tile([P, G], F32, "ratio")
        nc.gpsimd.tensor_tensor(ratio[:], pb[:], inv[:, 0:G], ALU.mult)
        gain_z = tile([P, 1], F32, "gain_z")
        nc.scalar.activation(gain_z[:], inv[:, G:G + 1], ACT.Copy, scale=gain[:])
        neg_z = tile([P, 1], F32, "neg_z")
        nc.scalar.activation(neg_z[:], inv[:, G:G + 1], ACT.Copy, scale=-1.0)
        num = tile([P, G], F32, "num")
        nc.vector.tensor_reduce(num[:], pa[:].rearrange("p (g r) -> p g r", r=PAGE), AX.X, ALU.add)
        part = tile([P, G], F32, "part")
        total = tile([P, 1], F32, "total")
        nc.vector.scalar_tensor_tensor(part[:], num[:], gain_z[:], ratio[:], ALU.mult, ALU.mult, accum_out=total[:])
        back = tile([P, G], F32, "back")
        nc.vector.tensor_scalar(back[:], pb[:], total[:], neg_z[:], ALU.mult, ALU.mult)
        nc.vector.tensor_tensor(gf[:].indirect(lst2[:]), part[:], back[:], ALU.add)
        res = tile([P, U], F32, "res")
        for h, queue in enumerate((nc.sync, nc.scalar)):
            cols = slice(h * U // 2, (h + 1) * U // 2)
            nc.vector.tensor_tensor(res[:, cols], old_sb[:, cols], gf[:, cols], ALU.add)
            queue.dma_start(out=out[:, cols], in_=res[:, cols])
